import numpy as np
import ml_dtypes


def mxq(x, axis, fmt="e4m3"):
    dtype, down = {"e4m3": (ml_dtypes.float8_e4m3fn, 7), "e5m2": (ml_dtypes.float8_e5m2, 14)}[fmt]
    v = np.moveaxis(np.asarray(x, np.float32).astype(ml_dtypes.bfloat16).astype(np.float64), axis, -1)
    blocks = v.reshape(v.shape[:-1] + (-1, 32))
    amax = np.abs(blocks).max(-1, keepdims=True)
    byte = np.maximum(np.where(amax > 0, np.frexp(amax)[1] - 1 + 127, 0) - down, 1)
    scale = np.exp2(byte - 127.0)
    codes = (blocks / scale).astype(np.float32).astype(dtype).astype(np.float64)
    return np.moveaxis((codes * scale).reshape(v.shape), -1, axis)


WIDE = False


def mx_kscale(k):
    if not WIDE:
        return np.ones(k)
    levels = np.array([10, -10, 5, -5, 0])
    if k % 512:
        return np.exp2(np.random.permutation(np.resize(levels, k // 32))).repeat(32)
    a = np.empty((k // 512, 16))
    for p in range(k // 512):
        a[p, :8] = np.random.permutation(np.resize(levels, 8))
        for g in range(8):
            far = levels[np.abs(levels - a[p, g]) >= 10]
            a[p, g + 8] = far[np.random.randint(len(far))]
    return np.exp2(a.ravel()).repeat(32)


def f64(x):
    return np.asarray(x).astype(np.float64)


def striped(idx):
    return np.tile(idx.reshape(-1, 16).T, (8, 1)).astype(np.uint16)


def unstriped(offs):
    return offs[:16].T.reshape(-1).astype(np.int64)


E2M1 = np.array([0.0, 0.5, 1.0, 1.5, 2.0, 3.0, 4.0, 6.0, -0.0, -0.5, -1.0, -1.5, -2.0, -3.0, -4.0, -6.0])


def pack_weight(w, fmt):
    k, n = w.shape
    w = f64(np.asarray(w, np.float32).astype(ml_dtypes.bfloat16)).reshape(k // 32, 32, n)
    amax = np.abs(w).max(1)
    if fmt == "e4m3":
        byte = np.frexp(amax)[1] - 1 + 127 - 7
    else:
        mant, ex = np.frexp(amax / 6.0)
        byte = np.where(mant > 0.5, ex, ex - 1) + 127
    byte = np.clip(np.where(amax > 0, byte, 1), 1, 254)
    scaled = (w * np.exp2(127.0 - byte)[:, None, :]).reshape(k, n).astype(np.float32)
    by_word = np.ascontiguousarray(scaled.reshape(k // 512, 128, 4, n).transpose(0, 1, 3, 2))
    if fmt == "e4m3":
        words = by_word.astype(ml_dtypes.float8_e4m3fn).view(np.uint8)
    else:
        c = by_word.astype(ml_dtypes.float4_e2m1fn).view(np.uint8) & 0xF
        words = (c[..., 0::2] | (c[..., 1::2] << 4)).reshape(k // 512, 128, 2 * n)
    return np.ascontiguousarray(words), np.ascontiguousarray(byte.astype(np.uint8).reshape(k // 512, 16, n))


def unpack_weight(words, scales, fmt):
    g, _, n = scales.shape
    words = np.ascontiguousarray(words).reshape(g, 128, n, -1)
    if fmt == "e4m3":
        vals = words.view(ml_dtypes.float8_e4m3fn).astype(np.float64)
    else:
        nib = np.empty((g, 128, n, 4), np.uint8)
        nib[..., 0::2] = words & 0xF
        nib[..., 1::2] = words >> 4
        vals = E2M1[nib]
    vals = vals * np.repeat(np.exp2(scales.astype(np.float64) - 127.0), 8, axis=1)[..., None]
    return vals.transpose(0, 1, 3, 2).reshape(g * 512, n)


def gelu(v):
    return 0.5 * v * (1.0 + np.tanh(np.sqrt(2.0 / np.pi) * (v + 0.044715 * v**3)))


def striped8(idx):
    return np.concatenate([v.reshape(-1, 16).T for v in idx]).astype(np.uint16)


def unstriped8(offs):
    return np.stack([offs[16 * g:16 * g + 16].T.reshape(-1) for g in range(8)]).astype(np.int64)


def runs(v, idx8):
    k = np.arange(v.shape[0])
    return v[k[:, None], idx8[k % 512 // 64]]


K, T, S, P, H, N = 1024, 2048, 1024, 512, 1024, 384


def setup_inputs():
    n = np.random.standard_normal
    s = mx_kscale(K)[:, None]
    u = mx_kscale(H)[:, None]
    d = {}
    d["tab_words"], d["tab_scales"] = pack_weight(n((K, T)) * s, "e4m3")
    d["offs"] = striped8(np.stack([np.random.permutation(T)[:S] for _ in range(8)]))
    d["w4_words"], d["w4_scales"] = pack_weight(1.2 * n((K, H)) / s / K ** 0.5, "e2m1")
    d["gain"] = (np.exp(0.3 * n(H)) * u[:, 0]).astype(np.float32)
    d["pos1"] = striped(np.random.permutation(S)[:P])
    d["pos2"] = striped(np.random.permutation(S)[:P])
    wc = n((H, N))
    wc = wc - wc.mean(axis=0)
    d["wc"] = (0.63 * wc / u / H ** 0.5).astype(np.float32)
    d["w8_words"], d["w8_scales"] = pack_weight(0.4 * n((H, N)) / u / H ** 0.5, "e4m3")
    d["bias"] = (0.5 * n(N)).astype(np.float32)
    return d


def reference(tab_words, tab_scales, offs, w4_words, w4_scales, gain, pos1, pos2, wc, w8_words, w8_scales, bias):
    v = runs(unpack_weight(tab_words, tab_scales, "e4m3"), unstriped8(offs))
    w4 = unpack_weight(w4_words, w4_scales, "e2m1")
    x = w4.T @ v
    h = f64(gain)[:, None] * (x / (1.0 + np.exp(-x)))
    size = np.abs(h)
    z = size[:, unstriped(pos1)] + size[:, unstriped(pos2)]
    zq = mxq(z, 0, "e4m3")
    phase = mxq(f64(wc), 0, "e4m3").T @ zq
    w8 = unpack_weight(w8_words, w8_scales, "e4m3")
    level = w8.T @ zq
    return np.cos(phase) + level + f64(bias)[:, None]

@@ -1,0 +1,259 @@
+import math
+from contextlib import ExitStack
+
+import concourse.mybir as mybir
+
+K, T, S, M, H, N = 1024, 2048, 1024, 512, 1024, 384
+FLOPS = 2 * K * H * S + 2 * 2 * H * N * M
+
+F32 = mybir.dt.float32
+BF16 = mybir.dt.bfloat16
+I32 = mybir.dt.int32
+U32 = mybir.dt.uint32
+U16 = mybir.dt.uint16
+U8 = mybir.dt.uint8
+FP8X4 = mybir.dt.float8_e4m3fn_x4
+FP4X4 = mybir.dt.float4_e2m1fn_x4
+ACT = mybir.ActivationFunctionType
+ALU = mybir.AluOpType
+
+P = 128
+BANK = 512
+WC_BYTES = 4 * N * 4
+CHUNKS = ((0, 256), (256, 512))
+
+
+def tile_list_reach_balance_features_kernel(
+    tc, tab_words, tab_scales, offs, w4_words, w4_scales, gain, pos1, pos2, wc, w8_words, w8_scales, bias, out
+):
+    nc = tc.nc
+    with ExitStack() as ctx:
+        keep = ctx.enter_context(tc.tile_pool(name="keep", bufs=1))
+        stage = ctx.enter_context(tc.tile_pool(name="stage", bufs=1))
+        ring = ctx.enter_context(tc.tile_pool(name="ring", bufs=3))
+        psum = ctx.enter_context(tc.psum_pool(name="psum", bufs=1))
+
+        def held(shape, dtype, name):
+            return keep.tile(shape, dtype, name=name, align_bytes=64)
+
+        offs_sb = keep.tile([P, S // 16], U16, name="offs_sb")
+        pos_sb = [keep.tile([P, M // 16], U16, name="pos_sb%d" % i) for i in range(2)]
+        banks = [psum.tile([P, BANK], F32, name="bank%d" % i) for i in range(8)]
+
+        ts_win = held([P, T // 4], I32, "ts_win")
+        w4s_raw = keep.tile([P, 2 * H // 4], I32, name="w4s_raw", tag="w4s_then_w8s", align_bytes=64)
+        v_scale = [held([P, S // 4], I32, "v_scale%d" % a) for a in range(2)]
+        nc.gpsimd.memset(ts_win[:], 0)
+        nc.vector.memset(w4s_raw[:], 0)
+        nc.vector.memset(v_scale[1][:], 0)
+
+        warm = held([P, 1], F32, "warm")
+        warm2 = held([P, 1], F32, "warm2")
+        nc.vector.memset(warm[:], 0.0)
+        nc.scalar.activation(warm2[:], warm[:], ACT.Silu)
+
+        gain_sb = held([P, 2, 4], F32, "gain_sb")
+        bias_sb = held([P, 3], F32, "bias_sb")
+        nc.sync.dma_start(offs_sb[:], offs)
+        ts32 = tab_scales.bitcast(I32)
+        for e in range(2):
+            nc.sync.dma_start(ts_win[e:P:16, :], ts32[0, e:16:2, :])
+        nc.sync.dma_start(ts_win[4:P:8, :], ts32[1])
+        w4_raw = [
+            stage.tile([P, 2, 256], I32, name="w4_raw%d" % b, offset=(0, 2 * WC_BYTES - 1024)[b]) for b in range(2)
+        ]
+        w4w32 = w4_words.bitcast(I32)
+        tw32 = tab_words.rearrange("a p t i -> a p (t i)").bitcast(I32)
+        tw_win = [keep.tile([P, T], I32, name="tw_win%d" % a, tag="tw%d" % a, align_bytes=64) for a in range(2)]
+        nc.sync.dma_start(w4_raw[0][:], w4w32[:, :, 0:256].rearrange("a p c -> p a c"))
+        nc.sync.dma_start(tw_win[0][:], tw32[0])
+        nc.sync.dma_start(tw_win[1][:], tw32[1])
+        w4s32 = w4_scales.bitcast(I32)
+        for d in range(4):
+            nc.sync.dma_start(
+                w4s_raw[32 * d : 32 * d + 4, :].rearrange("r (a c) -> r a c", a=2),
+                w4s32[:, 4 * d : 4 * d + 4, :].rearrange("a r c -> r a c"),
+            )
+        nc.sync.dma_start(pos_sb[0][:], pos1)
+        nc.sync.dma_start(pos_sb[1][:], pos2)
+        nc.sync.dma_start(gain_sb[:], gain.rearrange("(b p t) -> p b t", b=2, t=4))
+        with nc.allow_non_contiguous_dma(reason="one value a partition"):
+            nc.sync.dma_start(bias_sb[:], bias.rearrange("(c p) -> p c", p=P))
+        nc.sync.dma_start(w4_raw[1][:], w4w32[:, :, 256:512].rearrange("a p c -> p a c"))
+
+        ts_got = held([P, S // 4], I32, "ts_got")
+        nc.vector.tensor_copy(ts_got[:].bitcast(U8), ts_win[:].bitcast(U8).indirect(offs_sb[:]))
+        nc.vector.tensor_copy(v_scale[0][:], ts_got[:])
+        for e in range(2):
+            nc.scalar.dma_start(v_scale[0][2 + e : P : 32, :], ts_got[16 + e : P : 32, :])
+        for r in range(4):
+            nc.scalar.dma_start(v_scale[1][r:P:32, :], ts_got[8 * r + 4 : P : 32, :])
+
+        w4 = [held([P, 2 * 256], I32, "w4_%d" % b) for b in range(2)]
+        w4s = []
+
+        def deal_w4(b):
+            w4s.append(keep.tile([P, 2 * 128], I32, name="w4s_%d" % b, tag=("w4s0", "tw1")[b], align_bytes=64))
+            nc.vector.tensor_copy(
+                w4[b][:].bitcast(U16).rearrange("p (a t c i) -> p a c t i", a=2, t=4, i=8),
+                w4_raw[b][:].bitcast(U16).rearrange("p a (c i t) -> p a c t i", t=4, i=8),
+            )
+            nc.vector.tensor_copy(
+                w4s[b][:].bitcast(U8).rearrange("p (a t c i) -> p a c t i", a=2, t=4, i=16),
+                w4s_raw[:].bitcast(U8).rearrange("p (a b c i t) -> p b a c t i", a=2, b=2, t=4, i=16)[:, b],
+            )
+
+        deal_w4(0)
+        v = [[held([P, BANK], I32, "v%d_%d" % (a, j)) for j in range(2)] for a in range(2)]
+        for a in range(2):
+            for j in range(2):
+                nc.vector.tensor_copy(
+                    v[a][j][:].bitcast(U32), tw_win[a][:].bitcast(U32).indirect(offs_sb[:, 32 * j : 32 * (j + 1)])
+                )
+        deal_w4(1)
+
+        wc_raw = [stage.tile([P, 4, N], F32, name="wc_raw%d" % b, offset=b * WC_BYTES) for b in range(2)]
+        w8 = stage.tile([P, 2, N], I32, name="w8", offset=2 * WC_BYTES, align_bytes=64)
+        w8s = keep.tile([P, 2 * N // 4], I32, name="w8s", tag="w4s_then_w8s", align_bytes=64)
+        for b in range(2):
+            nc.sync.dma_start(wc_raw[b][:], wc[512 * b : 512 * (b + 1), :].rearrange("(p j) n -> p j n", j=4))
+        nc.sync.dma_start(w8[:], w8_words.rearrange("a p n i -> p a (n i)").bitcast(I32))
+        nc.gpsimd.memset(w8s[:], 0)
+        w8s32 = w8_scales.bitcast(I32)
+        for d in range(4):
+            nc.sync.dma_start(
+                w8s[32 * d : 32 * d + 4, :].rearrange("r (a c) -> r a c", a=2),
+                w8s32[:, 4 * d : 4 * d + 4, :].rearrange("a r c -> r a c"),
+            )
+
+        wc_bf = held([P, 2 * N * 4], BF16, "wc_bf")
+        wc_q = held([P, 2 * N], U32, "wc_q")
+        wc_s = held([P, 2 * N], U8, "wc_s")
+
+        def weave_wc(b):
+            nc.scalar.copy(
+                wc_bf[:, b * 4 * N : (b + 1) * 4 * N].rearrange("p (c i t) -> p c t i", i=4, t=4),
+                wc_raw[b][:].rearrange("p t (c i) -> p c t i", i=4),
+            )
+
+        def quantize_wc(b):
+            for c0, c1 in ((b * N, b * N + 256), (b * N + 256, (b + 1) * N)):
+                nc.vector.quantize_mx(wc_q[:, c0:c1].bitcast(FP8X4), wc_s[:, c0:c1], wc_bf[:, 4 * c0 : 4 * c1])
+
+        h = [held([P, S], F32, "h%d" % i) for i in range(8)]
+
+        def first_stage(i):
+            b, t = divmod(i, 4)
+            for j in range(2):
+                bank = banks[(2 * i + j) % 8]
+                for a in range(2):
+                    nc.tensor.matmul_mx(
+                        bank[:],
+                        lhsT=w4[b][:].bitcast(U8)[:, (4 * a + t) * 256 : (4 * a + t + 1) * 256].bitcast(FP4X4),
+                        lhsT_scale=w4s[b][:].bitcast(U8)[:, (4 * a + t) * 128 : (4 * a + t + 1) * 128],
+                        rhs=v[a][j][:].bitcast(FP8X4),
+                        rhs_scale=v_scale[a][:].bitcast(U8)[:, BANK * j : BANK * (j + 1)],
+                        start=(a == 0),
+                        stop=(a == 1),
+                    )
+                silu = ring.tile([P, BANK], F32, name="silu")
+                nc.scalar.activation(silu[:], bank[:], ACT.Silu)
+                nc.scalar.activation(h[i][:, BANK * j : BANK * (j + 1)], silu[:], ACT.Abs, scale=gain_sb[:, b, t : t + 1])
+
+        legs = [[held([P, 4, M], F32, "leg%d_%d" % (b, s)) for s in range(2)] for b in range(2)]
+        z_bf = [held([P, 4 * M], BF16, "z_bf%d" % b) for b in range(2)]
+        z_q = [held([P, M], U32, "z_q%d" % b) for b in range(2)]
+        z_s = [held([P, M], U8, "z_s%d" % b) for b in range(2)]
+
+        def pick(i, m0, m1):
+            b, t = divmod(i, 4)
+            for s in range(2):
+                nc.vector.tensor_copy(legs[b][s][:, t, m0:m1], h[i][:].indirect(pos_sb[s][:, m0 // 16 : m1 // 16]))
+
+        def add_legs(b, m0, m1):
+            nc.vector.tensor_tensor(
+                z_bf[b][:, 4 * m0 : 4 * m1].rearrange("p (c i t) -> p c t i", i=4, t=4),
+                legs[b][0][:, :, m0:m1].rearrange("p t (c i) -> p c t i", i=4),
+                legs[b][1][:, :, m0:m1].rearrange("p t (c i) -> p c t i", i=4),
+                ALU.add,
+            )
+
+        def quantize_z(b, m0, m1):
+            nc.vector.quantize_mx(z_q[b][:, m0:m1].bitcast(FP8X4), z_s[b][:, m0:m1], z_bf[b][:, 4 * m0 : 4 * m1])
+
+        def region(c, kind, n):
+            width = CHUNKS[c][1] - CHUNKS[c][0]
+            bank = banks[4 * c + 2 * kind + n // 2]
+            return bank[:, (n % 2) * width : (n % 2 + 1) * width]
+
+        def second_stage(c, b):
+            m0, m1 = CHUNKS[c]
+            for kind in range(2):
+                codes = wc_q[:] if kind == 0 else w8[:].rearrange("p a n -> p (a n)")
+                scales = wc_s[:] if kind == 0 else w8s[:].bitcast(U8)
+                for n in range(3):
+                    cols = slice(b * N + n * P, b * N + (n + 1) * P)
+                    nc.tensor.matmul_mx(
+                        region(c, kind, n),
+                        lhsT=codes[:, cols].bitcast(FP8X4),
+                        lhsT_scale=scales[:, cols],
+                        rhs=z_q[b][:, m0:m1].bitcast(FP8X4),
+                        rhs_scale=z_s[b][:, m0:m1],
+                        start=(b == 0 and n != 1),
+                        stop=(b == 1 and n != 0),
+                    )
+
+        def finish(c):
+            m0, m1 = CHUNKS[c]
+            width = m1 - m0
+            res = held([P, 3, width], F32, "res%d" % c)
+            cosine = held([P, 3 * width], F32, "cosine%d" % c)
+            for half, count in ((0, 2), (1, 1)):
+                phase = banks[4 * c + half][:, 0 : count * width]
+                turns = ring.tile([P, count * width], I32, name="turns")
+                rest = ring.tile([P, count * width], F32, name="rest")
+                size = ring.tile([P, count * width], F32, name="size")
+                if c == 0:
+                    whole = ring.tile([P, count * width], F32, name="whole")
+                    nc.scalar.activation(turns[:].bitcast(U32), phase, ACT.Abs, scale=1.0 / (2.0 * math.pi))
+                    nc.scalar.activation(whole[:], phase, ACT.Abs)
+                    nc.vector.scalar_tensor_tensor(rest[:], turns[:], -2.0 * math.pi, whole[:], ALU.mult, ALU.add)
+                else:
+                    nc.vector.tensor_scalar(turns[:], phase, 1.0 / (2.0 * math.pi), None, ALU.mult)
+                    nc.vector.scalar_tensor_tensor(rest[:], turns[:], -2.0 * math.pi, phase, ALU.mult, ALU.add)
+                nc.scalar.activation(size[:], rest[:], ACT.Abs)
+                nc.scalar.activation(
+                    cosine[:, 2 * half * width : (2 * half + count) * width], size[:], ACT.Sin, bias=math.pi / 2.0, scale=-1.0
+                )
+            for n in range(3):
+                nc.vector.scalar_tensor_tensor(
+                    res[:, n, :], region(c, 1, n), bias_sb[:, n : n + 1], cosine[:, n * width : (n + 1) * width], ALU.add, ALU.add
+                )
+            nc.sync.dma_start(out[:, m0:m1].rearrange("(c p) m -> p c m", p=P), res[:])
+
+        for i in range(4):
+            first_stage(i)
+            pick(i, 0, M)
+        weave_wc(0)
+        add_legs(0, 0, M)
+        first_stage(4)
+        pick(4, 0, M)
+        quantize_z(0, 0, M)
+        quantize_wc(0)
+        first_stage(5)
+        pick(5, 0, M)
+        first_stage(6)
+        first_stage(7)
+        weave_wc(1)
+        for c in range(2):
+            second_stage(c, 0)
+        for c, (m0, m1) in enumerate(CHUNKS):
+            pick(6, m0, m1)
+            pick(7, m0, m1)
+            add_legs(1, m0, m1)
+            if c == 0:
+                quantize_wc(1)
+            quantize_z(1, m0, m1)
+            second_stage(c, 1)
+        for c in range(2):
+            finish(c)

@@ -19,8 +19,10 @@ ALU = mybir.AluOpType
 
 P = 128
 BANK = 512
+HALF = M // 2
 WC_BYTES = 4 * N * 4
-CHUNKS = ((0, 256), (256, 512))
+W4_BYTES = 2048
+SECOND = 2 * WC_BYTES
 
 
 def tile_list_reach_balance_features_kernel(
@@ -33,15 +35,15 @@ def tile_list_reach_balance_features_kernel(
         ring = ctx.enter_context(tc.tile_pool(name="ring", bufs=3))
         psum = ctx.enter_context(tc.psum_pool(name="psum", bufs=1))
 
-        def held(shape, dtype, name):
-            return keep.tile(shape, dtype, name=name, align_bytes=64)
+        def held(shape, dtype, name, tag=""):
+            return keep.tile(shape, dtype, name=name, tag=tag, align_bytes=64)
 
         offs_sb = keep.tile([P, S // 16], U16, name="offs_sb")
         pos_sb = [keep.tile([P, M // 16], U16, name="pos_sb%d" % i) for i in range(2)]
         banks = [psum.tile([P, BANK], F32, name="bank%d" % i) for i in range(8)]
 
-        ts_win = held([P, T // 4], I32, "ts_win")
-        w4s_raw = keep.tile([P, 2 * H // 4], I32, name="w4s_raw", tag="w4s_then_w8s", align_bytes=64)
+        ts_win = stage.tile([P, T // 4], I32, name="ts_win", offset=WC_BYTES - 512, align_bytes=64)
+        w4s_raw = held([P, 2 * H // 4], I32, "w4s_raw", "w4s_then_w8s")
         v_scale = [held([P, S // 4], I32, "v_scale%d" % a) for a in range(2)]
         nc.gpsimd.memset(ts_win[:], 0)
         nc.vector.memset(w4s_raw[:], 0)
@@ -52,23 +54,23 @@ def tile_list_reach_balance_features_kernel(
         nc.vector.memset(warm[:], 0.0)
         nc.scalar.activation(warm2[:], warm[:], ACT.Silu)
 
-        gain_sb = held([P, 2, 4], F32, "gain_sb")
-        bias_sb = held([P, 3], F32, "bias_sb")
-        nc.sync.dma_start(offs_sb[:], offs)
+        w4_raw = [held([P, 2, 256], I32, "w4_raw0")]
+        w4w32 = w4_words.bitcast(I32)
+        w4s32 = w4_scales.bitcast(I32)
         ts32 = tab_scales.bitcast(I32)
+        tw32 = tab_words.rearrange("a p t i -> a p (t i)").bitcast(I32)
+        tw_win = [held([P, T], I32, "tw_win%d" % a, "tw%d" % a) for a in range(2)]
+        wc_raw = []
+
+        def load_wc(b):
+            nc.sync.dma_start(wc_raw[b][:], wc[512 * b : 512 * (b + 1), :].rearrange("(p j) n -> p j n", j=4))
+
+        nc.sync.dma_start(offs_sb[:], offs)
         for e in range(2):
             nc.sync.dma_start(ts_win[e:P:16, :], ts32[0, e:16:2, :])
         nc.sync.dma_start(ts_win[4:P:8, :], ts32[1])
-        w4_raw = [
-            stage.tile([P, 2, 256], I32, name="w4_raw%d" % b, offset=(0, 2 * WC_BYTES - 1024)[b]) for b in range(2)
-        ]
-        w4w32 = w4_words.bitcast(I32)
-        tw32 = tab_words.rearrange("a p t i -> a p (t i)").bitcast(I32)
-        tw_win = [keep.tile([P, T], I32, name="tw_win%d" % a, tag="tw%d" % a, align_bytes=64) for a in range(2)]
         nc.sync.dma_start(w4_raw[0][:], w4w32[:, :, 0:256].rearrange("a p c -> p a c"))
         nc.sync.dma_start(tw_win[0][:], tw32[0])
-        nc.sync.dma_start(tw_win[1][:], tw32[1])
-        w4s32 = w4_scales.bitcast(I32)
         for d in range(4):
             nc.sync.dma_start(
                 w4s_raw[32 * d : 32 * d + 4, :].rearrange("r (a c) -> r a c", a=2),
@@ -76,47 +78,63 @@ def tile_list_reach_balance_features_kernel(
             )
         nc.sync.dma_start(pos_sb[0][:], pos1)
         nc.sync.dma_start(pos_sb[1][:], pos2)
-        nc.sync.dma_start(gain_sb[:], gain.rearrange("(b p t) -> p b t", b=2, t=4))
-        with nc.allow_non_contiguous_dma(reason="one value a partition"):
-            nc.sync.dma_start(bias_sb[:], bias.rearrange("(c p) -> p c", p=P))
-        nc.sync.dma_start(w4_raw[1][:], w4w32[:, :, 256:512].rearrange("a p c -> p a c"))
+        nc.sync.dma_start(tw_win[1][:], tw32[1])
 
-        ts_got = held([P, S // 4], I32, "ts_got")
+        ts_got = stage.tile([P, S // 4], I32, name="ts_got", offset=SECOND + WC_BYTES - 512)
         nc.vector.tensor_copy(ts_got[:].bitcast(U8), ts_win[:].bitcast(U8).indirect(offs_sb[:]))
         nc.vector.tensor_copy(v_scale[0][:], ts_got[:])
-        for e in range(2):
-            nc.scalar.dma_start(v_scale[0][2 + e : P : 32, :], ts_got[16 + e : P : 32, :])
         for r in range(4):
-            nc.scalar.dma_start(v_scale[1][r:P:32, :], ts_got[8 * r + 4 : P : 32, :])
+            nc.sync.dma_start(v_scale[1][r:P:32, :], ts_got[8 * r + 4 : P : 32, :])
+        for e in range(2):
+            nc.sync.dma_start(v_scale[0][2 + e : P : 32, :], ts_got[16 + e : P : 32, :])
+        w4_raw.append(stage.tile([P, 2, 256], I32, name="w4_raw1", offset=WC_BYTES + 128))
+        wc_raw.append(stage.tile([P, 4, N], F32, name="wc_raw0", offset=0))
+        gain_sb = stage.tile([P, 2, 4], F32, name="gain_sb", offset=WC_BYTES)
+        nc.sync.dma_start(gain_sb[:], gain.rearrange("(b p t) -> p b t", b=2, t=4))
+        nc.sync.dma_start(w4_raw[1][:], w4w32[:, :, 256:512].rearrange("a p c -> p a c"))
+        load_wc(0)
 
         w4 = [held([P, 2 * 256], I32, "w4_%d" % b) for b in range(2)]
         w4s = []
 
-        def deal_w4(b):
-            w4s.append(keep.tile([P, 2 * 128], I32, name="w4s_%d" % b, tag=("w4s0", "tw1")[b], align_bytes=64))
+        def deal_w4_words(b):
             nc.vector.tensor_copy(
                 w4[b][:].bitcast(U16).rearrange("p (a t c i) -> p a c t i", a=2, t=4, i=8),
                 w4_raw[b][:].bitcast(U16).rearrange("p a (c i t) -> p a c t i", t=4, i=8),
             )
-            nc.vector.tensor_copy(
-                w4s[b][:].bitcast(U8).rearrange("p (a t c i) -> p a c t i", a=2, t=4, i=16),
-                w4s_raw[:].bitcast(U8).rearrange("p (a b c i t) -> p b a c t i", a=2, b=2, t=4, i=16)[:, b],
+
+        def deal_w4_scales(b):
+            w4s.append(held([P, 2 * 128], I32, "w4s_%d" % b, ""))
+            nc.gpsimd.tensor_copy(
+                w4s[b][:].bitcast(U8).rearrange("p (a t m) -> p a t m", a=2, t=4),
+                w4s_raw[:].bitcast(U8).rearrange("p (a b m t) -> p b a t m", a=2, b=2, t=4)[:, b],
             )
 
-        deal_w4(0)
-        v = [[held([P, BANK], I32, "v%d_%d" % (a, j)) for j in range(2)] for a in range(2)]
-        for a in range(2):
-            for j in range(2):
-                nc.vector.tensor_copy(
-                    v[a][j][:].bitcast(U32), tw_win[a][:].bitcast(U32).indirect(offs_sb[:, 32 * j : 32 * (j + 1)])
-                )
-        deal_w4(1)
+        deal_w4_words(0)
+        deal_w4_scales(0)
 
-        wc_raw = [stage.tile([P, 4, N], F32, name="wc_raw%d" % b, offset=b * WC_BYTES) for b in range(2)]
-        w8 = stage.tile([P, 2, N], I32, name="w8", offset=2 * WC_BYTES, align_bytes=64)
-        w8s = keep.tile([P, 2 * N // 4], I32, name="w8s", tag="w4s_then_w8s", align_bytes=64)
-        for b in range(2):
-            nc.sync.dma_start(wc_raw[b][:], wc[512 * b : 512 * (b + 1), :].rearrange("(p j) n -> p j n", j=4))
+        wc_raw.append(stage.tile([P, 4, N], F32, name="wc_raw1", offset=SECOND))
+        bias_sb = stage.tile([P, 3], F32, name="bias_sb", offset=SECOND + WC_BYTES)
+        load_wc(1)
+        with nc.allow_non_contiguous_dma(reason="one value a partition"):
+            nc.sync.dma_start(bias_sb[:], bias.rearrange("(c p) -> p c", p=P))
+
+        wc_bf = [held([P, N * 4], BF16, "wc_bf%d" % b) for b in range(2)]
+
+        def weave(engine_copy, dst, src):
+            engine_copy(dst.rearrange("p (c i t) -> p c t i", i=4, t=4), src.rearrange("p t (c i) -> p c t i", i=4))
+
+        v01 = stage.tile([P, BANK], I32, name="v0_1", offset=SECOND + WC_BYTES + 64, align_bytes=64)
+        v = [[held([P, BANK], I32, "v0_0"), v01], [held([P, BANK], I32, "v1_%d" % j) for j in range(2)]]
+        for a, j in ((0, 0), (1, 0), (1, 1), (0, 1)):
+            nc.vector.tensor_copy(
+                v[a][j][:].bitcast(U32), tw_win[a][:].bitcast(U32).indirect(offs_sb[:, 32 * j : 32 * (j + 1)])
+            )
+        deal_w4_words(1)
+        deal_w4_scales(1)
+
+        w8 = stage.tile([P, 2, N], I32, name="w8", offset=WC_BYTES + 128 + W4_BYTES - 64, align_bytes=64)
+        w8s = held([P, 2 * N // 4], I32, "w8s", "w4s_then_w8s")
         nc.sync.dma_start(w8[:], w8_words.rearrange("a p n i -> p a (n i)").bitcast(I32))
         nc.gpsimd.memset(w8s[:], 0)
         w8s32 = w8_scales.bitcast(I32)
@@ -126,25 +144,19 @@ def tile_list_reach_balance_features_kernel(
                 w8s32[:, 4 * d : 4 * d + 4, :].rearrange("a r c -> r a c"),
             )
 
-        wc_bf = held([P, 2 * N * 4], BF16, "wc_bf")
-        wc_q = held([P, 2 * N], U32, "wc_q")
+        wc_q = held([P, 2 * N], U32, "wc_q", "tw1")
         wc_s = held([P, 2 * N], U8, "wc_s")
 
-        def weave_wc(b):
-            nc.scalar.copy(
-                wc_bf[:, b * 4 * N : (b + 1) * 4 * N].rearrange("p (c i t) -> p c t i", i=4, t=4),
-                wc_raw[b][:].rearrange("p t (c i) -> p c t i", i=4),
-            )
-
         def quantize_wc(b):
-            for c0, c1 in ((b * N, b * N + 256), (b * N + 256, (b + 1) * N)):
-                nc.vector.quantize_mx(wc_q[:, c0:c1].bitcast(FP8X4), wc_s[:, c0:c1], wc_bf[:, 4 * c0 : 4 * c1])
+            for c0, c1 in ((0, 256), (256, N)):
+                cols = slice(b * N + c0, b * N + c1)
+                nc.vector.quantize_mx(wc_q[:, cols].bitcast(FP8X4), wc_s[:, cols], wc_bf[b][:, 4 * c0 : 4 * c1])
 
         h = [held([P, S], F32, "h%d" % i) for i in range(8)]
 
-        def first_stage(i):
+        def first_stage(i, scratch, halves=(0, 1)):
             b, t = divmod(i, 4)
-            for j in range(2):
+            for j in halves:
                 bank = banks[(2 * i + j) % 8]
                 for a in range(2):
                     nc.tensor.matmul_mx(
@@ -156,38 +168,26 @@ def tile_list_reach_balance_features_kernel(
                         start=(a == 0),
                         stop=(a == 1),
                     )
-                silu = ring.tile([P, BANK], F32, name="silu")
-                nc.scalar.activation(silu[:], bank[:], ACT.Silu)
-                nc.scalar.activation(h[i][:, BANK * j : BANK * (j + 1)], silu[:], ACT.Abs, scale=gain_sb[:, b, t : t + 1])
+                nc.scalar.activation(scratch[j], bank[:], ACT.Silu)
+                nc.scalar.activation(h[i][:, BANK * j : BANK * (j + 1)], scratch[j], ACT.Abs, scale=gain_sb[:, b, t : t + 1])
 
-        legs = [[held([P, 4, M], F32, "leg%d_%d" % (b, s)) for s in range(2)] for b in range(2)]
-        z_bf = [held([P, 4 * M], BF16, "z_bf%d" % b) for b in range(2)]
+        def pick_first(dst, i, m0, m1):
+            nc.vector.tensor_copy(dst, h[i][:].indirect(pos_sb[0][:, m0 // 16 : m1 // 16]))
+
+        def pick_second(dst, first, i, m0, m1):
+            nc.vector.tensor_tensor(dst, h[i][:].indirect(pos_sb[1][:, m0 // 16 : m1 // 16]), first, ALU.add)
+
         z_q = [held([P, M], U32, "z_q%d" % b) for b in range(2)]
         z_s = [held([P, M], U8, "z_s%d" % b) for b in range(2)]
 
-        def pick(i, m0, m1):
-            b, t = divmod(i, 4)
-            for s in range(2):
-                nc.vector.tensor_copy(legs[b][s][:, t, m0:m1], h[i][:].indirect(pos_sb[s][:, m0 // 16 : m1 // 16]))
-
-        def add_legs(b, m0, m1):
-            nc.vector.tensor_tensor(
-                z_bf[b][:, 4 * m0 : 4 * m1].rearrange("p (c i t) -> p c t i", i=4, t=4),
-                legs[b][0][:, :, m0:m1].rearrange("p t (c i) -> p c t i", i=4),
-                legs[b][1][:, :, m0:m1].rearrange("p t (c i) -> p c t i", i=4),
-                ALU.add,
-            )
-
-        def quantize_z(b, m0, m1):
-            nc.vector.quantize_mx(z_q[b][:, m0:m1].bitcast(FP8X4), z_s[b][:, m0:m1], z_bf[b][:, 4 * m0 : 4 * m1])
+        def quantize_z(b, m0, m1, src):
+            nc.vector.quantize_mx(z_q[b][:, m0:m1].bitcast(FP8X4), z_s[b][:, m0:m1], src)
 
         def region(c, kind, n):
-            width = CHUNKS[c][1] - CHUNKS[c][0]
-            bank = banks[4 * c + 2 * kind + n // 2]
-            return bank[:, (n % 2) * width : (n % 2 + 1) * width]
+            return banks[4 * c + 2 * kind + n // 2][:, (n % 2) * HALF : (n % 2 + 1) * HALF]
 
         def second_stage(c, b):
-            m0, m1 = CHUNKS[c]
+            m_cols = slice(c * HALF, (c + 1) * HALF)
             for kind in range(2):
                 codes = wc_q[:] if kind == 0 else w8[:].rearrange("p a n -> p (a n)")
                 scales = wc_s[:] if kind == 0 else w8s[:].bitcast(U8)
@@ -197,63 +197,83 @@ def tile_list_reach_balance_features_kernel(
                         region(c, kind, n),
                         lhsT=codes[:, cols].bitcast(FP8X4),
                         lhsT_scale=scales[:, cols],
-                        rhs=z_q[b][:, m0:m1].bitcast(FP8X4),
-                        rhs_scale=z_s[b][:, m0:m1],
+                        rhs=z_q[b][:, m_cols].bitcast(FP8X4),
+                        rhs_scale=z_s[b][:, m_cols],
                         start=(b == 0 and n != 1),
                         stop=(b == 1 and n != 0),
                     )
 
         def finish(c):
-            m0, m1 = CHUNKS[c]
-            width = m1 - m0
-            res = held([P, 3, width], F32, "res%d" % c)
-            cosine = held([P, 3 * width], F32, "cosine%d" % c)
-            for half, count in ((0, 2), (1, 1)):
-                phase = banks[4 * c + half][:, 0 : count * width]
-                turns = ring.tile([P, count * width], I32, name="turns")
-                rest = ring.tile([P, count * width], F32, name="rest")
-                size = ring.tile([P, count * width], F32, name="size")
+            res = held([P, 3, HALF], F32, "res%d" % c)
+            cosine = held([P, 3 * HALF], F32, "cosine%d" % c)
+            for pair, count in ((0, 2), (1, 1)):
+                phase = banks[4 * c + pair][:, 0 : count * HALF]
+                turns = ring.tile([P, count * HALF], I32, name="turns")
+                rest = ring.tile([P, count * HALF], F32, name="rest")
                 if c == 0:
-                    whole = ring.tile([P, count * width], F32, name="whole")
+                    size = ring.tile([P, count * HALF], F32, name="size")
+                    nc.scalar.activation(size[:], phase, ACT.Abs)
                     nc.scalar.activation(turns[:].bitcast(U32), phase, ACT.Abs, scale=1.0 / (2.0 * math.pi))
-                    nc.scalar.activation(whole[:], phase, ACT.Abs)
-                    nc.vector.scalar_tensor_tensor(rest[:], turns[:], -2.0 * math.pi, whole[:], ALU.mult, ALU.add)
+                    nc.vector.scalar_tensor_tensor(rest[:], turns[:], -2.0 * math.pi, size[:], ALU.mult, ALU.add)
                 else:
                     nc.vector.tensor_scalar(turns[:], phase, 1.0 / (2.0 * math.pi), None, ALU.mult)
                     nc.vector.scalar_tensor_tensor(rest[:], turns[:], -2.0 * math.pi, phase, ALU.mult, ALU.add)
-                nc.scalar.activation(size[:], rest[:], ACT.Abs)
+                folded = ring.tile([P, count * HALF], F32, name="folded")
+                nc.scalar.activation(folded[:], rest[:], ACT.Abs)
                 nc.scalar.activation(
-                    cosine[:, 2 * half * width : (2 * half + count) * width], size[:], ACT.Sin, bias=math.pi / 2.0, scale=-1.0
+                    cosine[:, 2 * pair * HALF : (2 * pair + count) * HALF], folded[:], ACT.Sin, bias=math.pi / 2.0, scale=-1.0
                 )
             for n in range(3):
                 nc.vector.scalar_tensor_tensor(
-                    res[:, n, :], region(c, 1, n), bias_sb[:, n : n + 1], cosine[:, n * width : (n + 1) * width], ALU.add, ALU.add
+                    res[:, n, :], region(c, 1, n), bias_sb[:, n : n + 1], cosine[:, n * HALF : (n + 1) * HALF], ALU.add, ALU.add
                 )
-            nc.sync.dma_start(out[:, m0:m1].rearrange("(c p) m -> p c m", p=P), res[:])
+                nc.sync.dma_start(out[n * P : (n + 1) * P, c * HALF : (c + 1) * HALF], res[:, n, :])
 
-        for i in range(4):
-            first_stage(i)
-            pick(i, 0, M)
-        weave_wc(0)
-        add_legs(0, 0, M)
-        first_stage(4)
-        pick(4, 0, M)
-        quantize_z(0, 0, M)
+        z0 = held([P, 4 * M], F32, "z0")
+        z0_bf_z1a = held([P, 2 * M + 4 * HALF], F32, "z0_bf_z1a")
+        z0_bf = z0_bf_z1a[:, 0 : 2 * M].bitcast(BF16)
+        z1a = z0_bf_z1a[:, 2 * M :]
+        sums = [z0[:, t * M : (t + 1) * M] for t in range(4)] + [z1a[:, t * HALF : (t + 1) * HALF] for t in range(4)]
+        silu = [held([P, BANK], F32, "silu%d" % j) for j in range(2)]
+        scratch = [(silu[0][:], silu[0][:]), (silu[1][:], sums[0])]
+        scratch.extend((silu[i % 2][:], sums[i - 1]) for i in range(2, 5))
+        for start in (2 * M - HALF, 2 * M + HALF, 2 * M + 2 * HALF):
+            scratch.append((silu[0][:], z0_bf_z1a[:, start : start + BANK]))
+        scratch[7] = (wc_bf[1][:].bitcast(F32)[:, 0:BANK], scratch[7][1])
+        first = []
+        weave(nc.vector.tensor_copy, wc_bf[0][:], wc_raw[0][:])
         quantize_wc(0)
-        first_stage(5)
-        pick(5, 0, M)
-        first_stage(6)
-        first_stage(7)
-        weave_wc(1)
+        first_stage(0, scratch[0], (0,))
+        first_stage(1, scratch[1], (0,))
+        for i in range(8):
+            width = M if i < 4 else HALF
+            first_stage(i, scratch[i], (1,) if i < 2 else (0, 1))
+            first.append(held([P, width], F32, "first%d" % i, "first%d" % (i % 3)))
+            pick_first(first[i][:], i, 0, width)
+            if i == 5:
+                weave(nc.vector.tensor_copy, z0_bf, z0[:].rearrange("p (t m) -> p t m", t=4))
+            if i > 0:
+                pick_second(sums[i - 1], first[i - 1][:], i - 1, 0, M if i - 1 < 4 else HALF)
+            if i == 5:
+                quantize_z(0, 0, M, z0_bf)
+        pick_second(sums[7], first[7][:], 7, 0, HALF)
+        weave(nc.scalar.copy, wc_bf[1][:], wc_raw[1][:])
         for c in range(2):
             second_stage(c, 0)
-        for c, (m0, m1) in enumerate(CHUNKS):
-            pick(6, m0, m1)
-            pick(7, m0, m1)
-            add_legs(1, m0, m1)
-            if c == 0:
-                quantize_wc(1)
-            quantize_z(1, m0, m1)
-            second_stage(c, 1)
+        z1a_bf = held([P, 4 * HALF], BF16, "z1a_bf", "z1a_bf_then_z1b")
+        weave(nc.scalar.copy, z1a_bf[:], z1a.rearrange("p (t m) -> p t m", t=4))
+        first_b = held([P, 4, HALF], F32, "first_b", "first0")
+        for i in range(4, 8):
+            pick_first(first_b[:, i % 4, :], i, HALF, M)
+        quantize_wc(1)
+        quantize_z(1, 0, HALF, z1a_bf[:])
+        second_stage(0, 1)
+        z1b = held([P, 4, HALF], F32, "z1b", "z1a_bf_then_z1b")
+        for i in range(4, 8):
+            pick_second(z1b[:, i % 4, :], first_b[:, i % 4, :], i, HALF, M)
+        z1b_bf = held([P, 4 * HALF], BF16, "z1b_bf")
+        weave(nc.scalar.copy, z1b_bf[:], z1b[:])
+        quantize_z(1, HALF, M, z1b_bf[:])
+        second_stage(1, 1)
         for c in range(2):
             finish(c)

@@ -119,7 +119,7 @@ def tile_list_reach_balance_features_kernel(
         with nc.allow_non_contiguous_dma(reason="one value a partition"):
             nc.sync.dma_start(bias_sb[:], bias.rearrange("(c p) -> p c", p=P))
 
-        wc_bf = [held([P, N * 4], BF16, "wc_bf%d" % b) for b in range(2)]
+        wc_bf = [held([P, N * 4], BF16, "wc_bf%d" % b)[:] for b in range(2)]
 
         def weave(engine_copy, dst, src):
             engine_copy(dst.rearrange("p (c i t) -> p c t i", i=4, t=4), src.rearrange("p t (c i) -> p c t i", i=4))
@@ -203,77 +203,81 @@ def tile_list_reach_balance_features_kernel(
                         stop=(b == 1 and n != 0),
                     )
 
+        cosine = [held([P, 3 * HALF], F32, "cosine%d" % c) for c in range(2)]
+
+        def cosines(c, pair):
+            width = (2 - pair) * HALF
+            phase = banks[4 * c + pair][:, 0:width]
+            turns = ring.tile([P, width], I32, name="turns")
+            rest = ring.tile([P, width], F32, name="rest")
+            folded = ring.tile([P, width], F32, name="folded")
+            if c == 0:
+                size = held([P, width], F32, "size%d_%d" % (c, pair), "size%d_%d" % (c, pair))
+                nc.scalar.activation(size[:], phase, ACT.Abs)
+                nc.scalar.activation(turns[:].bitcast(U32), phase, ACT.Abs, scale=1.0 / (2.0 * math.pi))
+                nc.vector.scalar_tensor_tensor(rest[:], turns[:], -2.0 * math.pi, size[:], ALU.mult, ALU.add)
+            else:
+                nc.vector.tensor_scalar(turns[:], phase, 1.0 / (2.0 * math.pi), None, ALU.mult)
+                nc.vector.scalar_tensor_tensor(rest[:], turns[:], -2.0 * math.pi, phase, ALU.mult, ALU.add)
+            nc.scalar.activation(folded[:], rest[:], ACT.Abs)
+            nc.scalar.activation(
+                cosine[c][:, 2 * pair * HALF : 2 * pair * HALF + width], folded[:], ACT.Sin, bias=math.pi / 2.0, scale=-1.0
+            )
+
         def finish(c):
-            res = held([P, 3, HALF], F32, "res%d" % c)
-            cosine = held([P, 3 * HALF], F32, "cosine%d" % c)
-            for pair, count in ((0, 2), (1, 1)):
-                phase = banks[4 * c + pair][:, 0 : count * HALF]
-                turns = ring.tile([P, count * HALF], I32, name="turns")
-                rest = ring.tile([P, count * HALF], F32, name="rest")
-                if c == 0:
-                    size = ring.tile([P, count * HALF], F32, name="size")
-                    nc.scalar.activation(size[:], phase, ACT.Abs)
-                    nc.scalar.activation(turns[:].bitcast(U32), phase, ACT.Abs, scale=1.0 / (2.0 * math.pi))
-                    nc.vector.scalar_tensor_tensor(rest[:], turns[:], -2.0 * math.pi, size[:], ALU.mult, ALU.add)
-                else:
-                    nc.vector.tensor_scalar(turns[:], phase, 1.0 / (2.0 * math.pi), None, ALU.mult)
-                    nc.vector.scalar_tensor_tensor(rest[:], turns[:], -2.0 * math.pi, phase, ALU.mult, ALU.add)
-                folded = ring.tile([P, count * HALF], F32, name="folded")
-                nc.scalar.activation(folded[:], rest[:], ACT.Abs)
-                nc.scalar.activation(
-                    cosine[:, 2 * pair * HALF : (2 * pair + count) * HALF], folded[:], ACT.Sin, bias=math.pi / 2.0, scale=-1.0
-                )
             for n in range(3):
+                res = ring.tile([P, HALF], F32, name="res", bufs=6)
                 nc.vector.scalar_tensor_tensor(
-                    res[:, n, :], region(c, 1, n), bias_sb[:, n : n + 1], cosine[:, n * HALF : (n + 1) * HALF], ALU.add, ALU.add
+                    res[:], region(c, 1, n), bias_sb[:, n : n + 1], cosine[c][:, n * HALF : (n + 1) * HALF], ALU.add, ALU.add
                 )
-                nc.sync.dma_start(out[n * P : (n + 1) * P, c * HALF : (c + 1) * HALF], res[:, n, :])
+                nc.sync.dma_start(out[n * P : (n + 1) * P, c * HALF : (c + 1) * HALF], res[:])
 
         z0 = held([P, 4 * M], F32, "z0")
-        z0_bf_z1a = held([P, 2 * M + 4 * HALF], F32, "z0_bf_z1a")
-        z0_bf = z0_bf_z1a[:, 0 : 2 * M].bitcast(BF16)
-        z1a = z0_bf_z1a[:, 2 * M :]
-        sums = [z0[:, t * M : (t + 1) * M] for t in range(4)] + [z1a[:, t * HALF : (t + 1) * HALF] for t in range(4)]
+        rows = held([P, 4, HALF + 2 * M], F32, "rows")
+        z0_bf = rows[:, 2, HALF:].bitcast(BF16)
+        sums = [z0[:, t * M : (t + 1) * M] for t in range(4)] + [rows[:, t, 0:HALF] for t in range(4)]
         silu = [held([P, BANK], F32, "silu%d" % j) for j in range(2)]
         scratch = [(silu[0][:], silu[0][:]), (silu[1][:], sums[0])]
         scratch.extend((silu[i % 2][:], sums[i - 1]) for i in range(2, 5))
-        for start in (2 * M - HALF, 2 * M + HALF, 2 * M + 2 * HALF):
-            scratch.append((silu[0][:], z0_bf_z1a[:, start : start + BANK]))
-        scratch[7] = (wc_bf[1][:].bitcast(F32)[:, 0:BANK], scratch[7][1])
+        scratch.extend((silu[i % 2][:], rows[:, i - 5, 0:BANK]) for i in range(5, 7))
+        scratch.append((wc_bf[1].bitcast(F32)[:, 0:BANK], rows[:, 2, 0:BANK]))
         first = []
-        weave(nc.vector.tensor_copy, wc_bf[0][:], wc_raw[0][:])
+        weave(nc.vector.tensor_copy, wc_bf[0], wc_raw[0][:])
         quantize_wc(0)
         first_stage(0, scratch[0], (0,))
         first_stage(1, scratch[1], (0,))
         for i in range(8):
-            width = M if i < 4 else HALF
             first_stage(i, scratch[i], (1,) if i < 2 else (0, 1))
-            first.append(held([P, width], F32, "first%d" % i, "first%d" % (i % 3)))
-            pick_first(first[i][:], i, 0, width)
-            if i == 5:
-                weave(nc.vector.tensor_copy, z0_bf, z0[:].rearrange("p (t m) -> p t m", t=4))
+            first.append(held([P, M], F32, "first%d" % i))
+            if i < 7:
+                pick_first(first[i][:], i, 0, M)
+            else:
+                pick_first(first[i][:, 0:HALF], i, 0, HALF)
             if i > 0:
-                pick_second(sums[i - 1], first[i - 1][:], i - 1, 0, M if i - 1 < 4 else HALF)
-            if i == 5:
-                quantize_z(0, 0, M, z0_bf)
-        pick_second(sums[7], first[7][:], 7, 0, HALF)
-        weave(nc.scalar.copy, wc_bf[1][:], wc_raw[1][:])
-        for c in range(2):
-            second_stage(c, 0)
-        z1a_bf = held([P, 4 * HALF], BF16, "z1a_bf", "z1a_bf_then_z1b")
-        weave(nc.scalar.copy, z1a_bf[:], z1a.rearrange("p (t m) -> p t m", t=4))
-        first_b = held([P, 4, HALF], F32, "first_b", "first0")
-        for i in range(4, 8):
-            pick_first(first_b[:, i % 4, :], i, HALF, M)
+                width = M if i - 1 < 4 else HALF
+                pick_second(sums[i - 1], first[i - 1][:, 0:width], i - 1, 0, width)
+        pick_second(sums[7], first[7][:, 0:HALF], 7, 0, HALF)
+        pick_first(first[7][:, HALF:M], 7, HALF, M)
+        weave(nc.scalar.copy, z0_bf, z0[:].rearrange("p (t m) -> p t m", t=4))
+        quantize_z(0, 0, M, z0_bf)
+        second_stage(0, 0)
+        second_stage(1, 0)
+        weave(nc.scalar.copy, wc_bf[1], wc_raw[1][:])
         quantize_wc(1)
+        z1a_bf = held([P, 4 * HALF], BF16, "z1a_bf", "z1a_bf_then_z1b")
+        weave(nc.scalar.copy, z1a_bf[:], rows[:, :, 0:HALF])
         quantize_z(1, 0, HALF, z1a_bf[:])
         second_stage(0, 1)
         z1b = held([P, 4, HALF], F32, "z1b", "z1a_bf_then_z1b")
         for i in range(4, 8):
-            pick_second(z1b[:, i % 4, :], first_b[:, i % 4, :], i, HALF, M)
+            pick_second(z1b[:, i % 4, :], first[i][:, HALF:M], i, HALF, M)
         z1b_bf = held([P, 4 * HALF], BF16, "z1b_bf")
-        weave(nc.scalar.copy, z1b_bf[:], z1b[:])
+        weave(nc.vector.tensor_copy, z1b_bf[:], z1b[:])
         quantize_z(1, HALF, M, z1b_bf[:])
         second_stage(1, 1)
-        for c in range(2):
-            finish(c)
+        cosines(0, 0)
+        cosines(0, 1)
+        cosines(1, 0)
+        cosines(1, 1)
+        finish(0)
+        finish(1)

import math
from contextlib import ExitStack

import concourse.mybir as mybir

K, T, S, M, H, N = 1024, 2048, 1024, 512, 1024, 384
FLOPS = 2 * K * H * S + 2 * 2 * H * N * M

F32 = mybir.dt.float32
BF16 = mybir.dt.bfloat16
I32 = mybir.dt.int32
U32 = mybir.dt.uint32
U16 = mybir.dt.uint16
U8 = mybir.dt.uint8
FP8X4 = mybir.dt.float8_e4m3fn_x4
FP4X4 = mybir.dt.float4_e2m1fn_x4
ACT = mybir.ActivationFunctionType
ALU = mybir.AluOpType

P = 128
BANK = 512
HALF = M // 2
WC_BYTES = 4 * N * 4
W4_BYTES = 2048
SECOND = 2 * WC_BYTES


def tile_list_reach_balance_features_kernel(
    tc, tab_words, tab_scales, offs, w4_words, w4_scales, gain, pos1, pos2, wc, w8_words, w8_scales, bias, out
):
    nc = tc.nc
    with ExitStack() as ctx:
        keep = ctx.enter_context(tc.tile_pool(name="keep", bufs=1))
        stage = ctx.enter_context(tc.tile_pool(name="stage", bufs=1))
        ring = ctx.enter_context(tc.tile_pool(name="ring", bufs=3))
        psum = ctx.enter_context(tc.psum_pool(name="psum", bufs=1))

        def held(shape, dtype, name, tag=""):
            return keep.tile(shape, dtype, name=name, tag=tag, align_bytes=64)

        offs_sb = keep.tile([P, S // 16], U16, name="offs_sb")
        pos_sb = [keep.tile([P, M // 16], U16, name="pos_sb%d" % i) for i in range(2)]
        banks = [psum.tile([P, BANK], F32, name="bank%d" % i) for i in range(8)]

        ts_win = stage.tile([P, T // 4], I32, name="ts_win", offset=WC_BYTES - 512, align_bytes=64)
        w4s_raw = held([P, 2 * H // 4], I32, "w4s_raw", "w4s_then_w8s")
        v_scale = [held([P, S // 4], I32, "v_scale%d" % a) for a in range(2)]
        nc.gpsimd.memset(ts_win[:], 0)
        nc.vector.memset(w4s_raw[:], 0)
        nc.vector.memset(v_scale[1][:], 0)

        warm = held([P, 1], F32, "warm")
        warm2 = held([P, 1], F32, "warm2")
        nc.vector.memset(warm[:], 0.0)
        nc.scalar.activation(warm2[:], warm[:], ACT.Silu)

        w4_raw = [held([P, 2, 256], I32, "w4_raw0")]
        w4w32 = w4_words.bitcast(I32)
        w4s32 = w4_scales.bitcast(I32)
        ts32 = tab_scales.bitcast(I32)
        tw32 = tab_words.rearrange("a p t i -> a p (t i)").bitcast(I32)
        tw_win = [held([P, T], I32, "tw_win%d" % a, "tw%d" % a) for a in range(2)]
        wc_raw = []

        def load_wc(b):
            nc.sync.dma_start(wc_raw[b][:], wc[512 * b : 512 * (b + 1), :].rearrange("(p j) n -> p j n", j=4))

        nc.sync.dma_start(offs_sb[:], offs)
        for e in range(2):
            nc.sync.dma_start(ts_win[e:P:16, :], ts32[0, e:16:2, :])
        nc.sync.dma_start(ts_win[4:P:8, :], ts32[1])
        nc.sync.dma_start(w4_raw[0][:], w4w32[:, :, 0:256].rearrange("a p c -> p a c"))
        nc.sync.dma_start(tw_win[0][:], tw32[0])
        for d in range(4):
            nc.sync.dma_start(
                w4s_raw[32 * d : 32 * d + 4, :].rearrange("r (a c) -> r a c", a=2),
                w4s32[:, 4 * d : 4 * d + 4, :].rearrange("a r c -> r a c"),
            )
        nc.sync.dma_start(pos_sb[0][:], pos1)
        nc.sync.dma_start(pos_sb[1][:], pos2)
        nc.sync.dma_start(tw_win[1][:], tw32[1])

        ts_got = stage.tile([P, S // 4], I32, name="ts_got", offset=SECOND + WC_BYTES - 512)
        nc.vector.tensor_copy(ts_got[:].bitcast(U8), ts_win[:].bitcast(U8).indirect(offs_sb[:]))
        nc.vector.tensor_copy(v_scale[0][:], ts_got[:])
        for r in range(4):
            nc.sync.dma_start(v_scale[1][r:P:32, :], ts_got[8 * r + 4 : P : 32, :])
        for e in range(2):
            nc.sync.dma_start(v_scale[0][2 + e : P : 32, :], ts_got[16 + e : P : 32, :])
        w4_raw.append(stage.tile([P, 2, 256], I32, name="w4_raw1", offset=WC_BYTES + 128))
        wc_raw.append(stage.tile([P, 4, N], F32, name="wc_raw0", offset=0))
        gain_sb = stage.tile([P, 2, 4], F32, name="gain_sb", offset=WC_BYTES)
        nc.sync.dma_start(gain_sb[:], gain.rearrange("(b p t) -> p b t", b=2, t=4))
        nc.sync.dma_start(w4_raw[1][:], w4w32[:, :, 256:512].rearrange("a p c -> p a c"))
        load_wc(0)

        w4 = [held([P, 2 * 256], I32, "w4_%d" % b) for b in range(2)]
        w4s = []

        def deal_w4_words(b):
            nc.vector.tensor_copy(
                w4[b][:].bitcast(U16).rearrange("p (a t c i) -> p a c t i", a=2, t=4, i=8),
                w4_raw[b][:].bitcast(U16).rearrange("p a (c i t) -> p a c t i", t=4, i=8),
            )

        def deal_w4_scales(b):
            w4s.append(held([P, 2 * 128], I32, "w4s_%d" % b, ""))
            nc.gpsimd.tensor_copy(
                w4s[b][:].bitcast(U8).rearrange("p (a t m) -> p a t m", a=2, t=4),
                w4s_raw[:].bitcast(U8).rearrange("p (a b m t) -> p b a t m", a=2, b=2, t=4)[:, b],
            )

        deal_w4_words(0)
        deal_w4_scales(0)

        wc_raw.append(stage.tile([P, 4, N], F32, name="wc_raw1", offset=SECOND))
        bias_sb = stage.tile([P, 3], F32, name="bias_sb", offset=SECOND + WC_BYTES)
        load_wc(1)
        with nc.allow_non_contiguous_dma(reason="one value a partition"):
            nc.sync.dma_start(bias_sb[:], bias.rearrange("(c p) -> p c", p=P))

        wc_bf = [held([P, N * 4], BF16, "wc_bf%d" % b)[:] for b in range(2)]

        def weave(engine_copy, dst, src):
            engine_copy(dst.rearrange("p (c i t) -> p c t i", i=4, t=4), src.rearrange("p t (c i) -> p c t i", i=4))

        v01 = stage.tile([P, BANK], I32, name="v0_1", offset=SECOND + WC_BYTES + 64, align_bytes=64)
        v = [[held([P, BANK], I32, "v0_0"), v01], [held([P, BANK], I32, "v1_%d" % j) for j in range(2)]]
        for a, j in ((0, 0), (1, 0), (1, 1), (0, 1)):
            nc.vector.tensor_copy(
                v[a][j][:].bitcast(U32), tw_win[a][:].bitcast(U32).indirect(offs_sb[:, 32 * j : 32 * (j + 1)])
            )
        deal_w4_words(1)
        deal_w4_scales(1)

        w8 = stage.tile([P, 2, N], I32, name="w8", offset=WC_BYTES + 128 + W4_BYTES - 64, align_bytes=64)
        w8s = held([P, 2 * N // 4], I32, "w8s", "w4s_then_w8s")
        nc.sync.dma_start(w8[:], w8_words.rearrange("a p n i -> p a (n i)").bitcast(I32))
        nc.gpsimd.memset(w8s[:], 0)
        w8s32 = w8_scales.bitcast(I32)
        for d in range(4):
            nc.sync.dma_start(
                w8s[32 * d : 32 * d + 4, :].rearrange("r (a c) -> r a c", a=2),
                w8s32[:, 4 * d : 4 * d + 4, :].rearrange("a r c -> r a c"),
            )

        wc_q = held([P, 2 * N], U32, "wc_q", "tw1")
        wc_s = held([P, 2 * N], U8, "wc_s")

        def quantize_wc(b):
            for c0, c1 in ((0, 256), (256, N)):
                cols = slice(b * N + c0, b * N + c1)
                nc.vector.quantize_mx(wc_q[:, cols].bitcast(FP8X4), wc_s[:, cols], wc_bf[b][:, 4 * c0 : 4 * c1])

        h = [held([P, S], F32, "h%d" % i) for i in range(8)]

        def first_stage(i, scratch, halves=(0, 1)):
            b, t = divmod(i, 4)
            for j in halves:
                bank = banks[(2 * i + j) % 8]
                for a in range(2):
                    nc.tensor.matmul_mx(
                        bank[:],
                        lhsT=w4[b][:].bitcast(U8)[:, (4 * a + t) * 256 : (4 * a + t + 1) * 256].bitcast(FP4X4),
                        lhsT_scale=w4s[b][:].bitcast(U8)[:, (4 * a + t) * 128 : (4 * a + t + 1) * 128],
                        rhs=v[a][j][:].bitcast(FP8X4),
                        rhs_scale=v_scale[a][:].bitcast(U8)[:, BANK * j : BANK * (j + 1)],
                        start=(a == 0),
                        stop=(a == 1),
                    )
                nc.scalar.activation(scratch[j], bank[:], ACT.Silu)
                nc.scalar.activation(h[i][:, BANK * j : BANK * (j + 1)], scratch[j], ACT.Abs, scale=gain_sb[:, b, t : t + 1])

        def pick_first(dst, i, m0, m1):
            nc.vector.tensor_copy(dst, h[i][:].indirect(pos_sb[0][:, m0 // 16 : m1 // 16]))

        def pick_second(dst, first, i, m0, m1):
            nc.vector.tensor_tensor(dst, h[i][:].indirect(pos_sb[1][:, m0 // 16 : m1 // 16]), first, ALU.add)

        z_q = [held([P, M], U32, "z_q%d" % b) for b in range(2)]
        z_s = [held([P, M], U8, "z_s%d" % b) for b in range(2)]

        def quantize_z(b, m0, m1, src):
            nc.vector.quantize_mx(z_q[b][:, m0:m1].bitcast(FP8X4), z_s[b][:, m0:m1], src)

        def region(c, kind, n):
            return banks[4 * c + 2 * kind + n // 2][:, (n % 2) * HALF : (n % 2 + 1) * HALF]

        def second_stage(c, b):
            m_cols = slice(c * HALF, (c + 1) * HALF)
            for kind in range(2):
                codes = wc_q[:] if kind == 0 else w8[:].rearrange("p a n -> p (a n)")
                scales = wc_s[:] if kind == 0 else w8s[:].bitcast(U8)
                for n in range(3):
                    cols = slice(b * N + n * P, b * N + (n + 1) * P)
                    nc.tensor.matmul_mx(
                        region(c, kind, n),
                        lhsT=codes[:, cols].bitcast(FP8X4),
                        lhsT_scale=scales[:, cols],
                        rhs=z_q[b][:, m_cols].bitcast(FP8X4),
                        rhs_scale=z_s[b][:, m_cols],
                        start=(b == 0 and n != 1),
                        stop=(b == 1 and n != 0),
                    )

        cosine = [held([P, 3 * HALF], F32, "cosine%d" % c) for c in range(2)]

        def cosines(c, pair):
            width = (2 - pair) * HALF
            phase = banks[4 * c + pair][:, 0:width]
            turns = ring.tile([P, width], I32, name="turns")
            rest = ring.tile([P, width], F32, name="rest")
            folded = ring.tile([P, width], F32, name="folded")
            if c == 0:
                size = held([P, width], F32, "size%d_%d" % (c, pair), "size%d_%d" % (c, pair))
                nc.scalar.activation(size[:], phase, ACT.Abs)
                nc.scalar.activation(turns[:].bitcast(U32), phase, ACT.Abs, scale=1.0 / (2.0 * math.pi))
                nc.vector.scalar_tensor_tensor(rest[:], turns[:], -2.0 * math.pi, size[:], ALU.mult, ALU.add)
            else:
                nc.vector.tensor_scalar(turns[:], phase, 1.0 / (2.0 * math.pi), None, ALU.mult)
                nc.vector.scalar_tensor_tensor(rest[:], turns[:], -2.0 * math.pi, phase, ALU.mult, ALU.add)
            nc.scalar.activation(folded[:], rest[:], ACT.Abs)
            nc.scalar.activation(
                cosine[c][:, 2 * pair * HALF : 2 * pair * HALF + width], folded[:], ACT.Sin, bias=math.pi / 2.0, scale=-1.0
            )

        def finish(c):
            for n in range(3):
                res = ring.tile([P, HALF], F32, name="res", bufs=6)
                nc.vector.scalar_tensor_tensor(
                    res[:], region(c, 1, n), bias_sb[:, n : n + 1], cosine[c][:, n * HALF : (n + 1) * HALF], ALU.add, ALU.add
                )
                nc.sync.dma_start(out[n * P : (n + 1) * P, c * HALF : (c + 1) * HALF], res[:])

        z0 = held([P, 4 * M], F32, "z0")
        rows = held([P, 4, HALF + 2 * M], F32, "rows")
        z0_bf = rows[:, 2, HALF:].bitcast(BF16)
        sums = [z0[:, t * M : (t + 1) * M] for t in range(4)] + [rows[:, t, 0:HALF] for t in range(4)]
        silu = [held([P, BANK], F32, "silu%d" % j) for j in range(2)]
        scratch = [(silu[0][:], silu[0][:]), (silu[1][:], sums[0])]
        scratch.extend((silu[i % 2][:], sums[i - 1]) for i in range(2, 5))
        scratch.extend((silu[i % 2][:], rows[:, i - 5, 0:BANK]) for i in range(5, 7))
        scratch.append((wc_bf[1].bitcast(F32)[:, 0:BANK], rows[:, 2, 0:BANK]))
        first = []
        weave(nc.vector.tensor_copy, wc_bf[0], wc_raw[0][:])
        quantize_wc(0)
        first_stage(0, scratch[0], (0,))
        first_stage(1, scratch[1], (0,))
        for i in range(8):
            first_stage(i, scratch[i], (1,) if i < 2 else (0, 1))
            first.append(held([P, M], F32, "first%d" % i))
            if i < 7:
                pick_first(first[i][:], i, 0, M)
            else:
                pick_first(first[i][:, 0:HALF], i, 0, HALF)
            if i > 0:
                width = M if i - 1 < 4 else HALF
                pick_second(sums[i - 1], first[i - 1][:, 0:width], i - 1, 0, width)
        pick_second(sums[7], first[7][:, 0:HALF], 7, 0, HALF)
        pick_first(first[7][:, HALF:M], 7, HALF, M)
        weave(nc.scalar.copy, z0_bf, z0[:].rearrange("p (t m) -> p t m", t=4))
        quantize_z(0, 0, M, z0_bf)
        second_stage(0, 0)
        second_stage(1, 0)
        weave(nc.scalar.copy, wc_bf[1], wc_raw[1][:])
        quantize_wc(1)
        z1a_bf = held([P, 4 * HALF], BF16, "z1a_bf", "z1a_bf_then_z1b")
        weave(nc.scalar.copy, z1a_bf[:], rows[:, :, 0:HALF])
        quantize_z(1, 0, HALF, z1a_bf[:])
        second_stage(0, 1)
        z1b = held([P, 4, HALF], F32, "z1b", "z1a_bf_then_z1b")
        for i in range(4, 8):
            pick_second(z1b[:, i % 4, :], first[i][:, HALF:M], i, HALF, M)
        z1b_bf = held([P, 4 * HALF], BF16, "z1b_bf")
        weave(nc.vector.tensor_copy, z1b_bf[:], z1b[:])
        quantize_z(1, HALF, M, z1b_bf[:])
        second_stage(1, 1)
        cosines(0, 0)
        cosines(0, 1)
        cosines(1, 0)
        cosines(1, 1)
        finish(0)
        finish(1)
